import numpy as np
import ml_dtypes


def mxq(x, axis, fmt="e4m3"):
    dtype, down = {"e4m3": (ml_dtypes.float8_e4m3fn, 7), "e5m2": (ml_dtypes.float8_e5m2, 14)}[fmt]
    v = np.moveaxis(np.asarray(x, np.float32).astype(ml_dtypes.bfloat16).astype(np.float64), axis, -1)
    blocks = v.reshape(v.shape[:-1] + (-1, 32))
    amax = np.abs(blocks).max(-1, keepdims=True)
    byte = np.maximum(np.where(amax > 0, np.frexp(amax)[1] - 1 + 127, 0) - down, 1)
    scale = np.exp2(byte - 127.0)
    codes = (blocks / scale).astype(np.float32).astype(dtype).astype(np.float64)
    return np.moveaxis((codes * scale).reshape(v.shape), -1, axis)


WIDE = False


def mx_kscale(k):
    if not WIDE:
        return np.ones(k)
    levels = np.array([10, -10, 5, -5, 0])
    if k % 512:
        return np.exp2(np.random.permutation(np.resize(levels, k // 32))).repeat(32)
    a = np.empty((k // 512, 16))
    for p in range(k // 512):
        a[p, :8] = np.random.permutation(np.resize(levels, 8))
        for g in range(8):
            far = levels[np.abs(levels - a[p, g]) >= 10]
            a[p, g + 8] = far[np.random.randint(len(far))]
    return np.exp2(a.ravel()).repeat(32)


BF16 = ml_dtypes.bfloat16


def bf(x):
    return np.asarray(x, np.float32).astype(BF16)


def f64(x):
    return np.asarray(x).astype(np.float64)


N, D, K, V = 512, 512, 4, 2048


def log_sum_exp(x, axis):
    m = np.max(x, axis=axis, keepdims=True)
    return m + np.log(np.sum(np.exp(x - m), axis=axis, keepdims=True))


def log_normalize(x, axis):
    s = x - np.max(x, axis=axis, keepdims=True)
    return s - np.log(np.sum(np.exp(s), axis=axis, keepdims=True))


def draw0():
    s = mx_kscale(D)
    t = mx_kscale(D)
    return {"h": bf(np.random.standard_normal((N, D)) * s),
            "w": bf(np.random.standard_normal((K, D, D)) / np.sqrt(D) / s[None, :, None]),
            "g": bf((1.0 + 0.1 * np.random.standard_normal((K, D))) * t),
            "u": bf(np.random.standard_normal((K, D)) * 2.0 / np.sqrt(D)),
            "emb": bf(np.random.standard_normal((V, D)) * 3.0 / np.sqrt(D) / t)}


def core(h, w, g, u, emb):
    n, d = h.shape
    k = w.shape[0]
    vocab = emb.shape[0]
    c = mxq(f64(h), 1, "e4m3") @ mxq(f64(w), 1, "e4m3")
    t = np.tanh(c.transpose(1, 0, 2))
    a = t * f64(g)[None, :, :]
    aq = mxq(a.reshape(n * k, d), 1, "e4m3")
    l = (aq @ mxq(f64(emb), 1, "e4m3").T).reshape(n, k, vocab)
    z = np.sum(t * f64(u)[None, :, :], axis=-1)
    logpi = log_normalize(z, axis=-1)
    lp = log_normalize(l, axis=-1)
    joint = logpi[:, :, None] + lp
    mixed = np.squeeze(log_sum_exp(joint, axis=1), axis=1)
    return mixed + np.log(vocab)


def e4m3fn_bytes(y):
    return np.clip(np.asarray(y, np.float64), -448.0, 448.0).astype(np.float32).astype(ml_dtypes.float8_e4m3fn).view(np.uint8)


def e4m3fn_values(b):
    return np.asarray(b, np.uint8).view(ml_dtypes.float8_e4m3fn).astype(np.float64)


def setup_inputs():
    d = draw0()
    x0 = np.asarray(d['w']).astype(np.float64)
    s = (np.max(np.abs(x0), axis=(0, 2), keepdims=True) / 448.0).astype(np.float32)
    out = {}
    for k, v in d.items():
        if k == 'w':
            out['w_bytes'] = e4m3fn_bytes(x0 / s.astype(np.float64))
            out['w_scale'] = s
        else:
            out[k] = v
    return out


def reference(h, w_bytes, w_scale, g, u, emb):
    return core(h, e4m3fn_values(w_bytes) * w_scale.astype(np.float64), g, u, emb)

@@ -1,0 +1,429 @@
+from contextlib import ExitStack
+
+import concourse.mybir as mybir
+from concourse.masks import make_identity
+
+N, D, K, V = 512, 512, 4, 2048
+FLOPS = 2 * N * D * K * D + 2 * N * K * D * V
+
+F32 = mybir.dt.float32
+BF16 = mybir.dt.bfloat16
+U32 = mybir.dt.uint32
+U8 = mybir.dt.uint8
+FP8 = mybir.dt.float8_e4m3fn
+FP8X4 = mybir.dt.float8_e4m3fn_x4
+ACT = mybir.ActivationFunctionType
+ALU = mybir.AluOpType
+AX = mybir.AxisListType
+
+P = 128
+T = 4
+NT = N // P
+CH = 512
+NJ = V // CH
+UNITS = NT * K
+ON_PE = ((3, 0, 3, 0), (3, 0, 3, 0), (3, 0, 3, 0), (1, 1, 1, 1))
+LAG = 9
+
+
+def tile_mixtureofsoftmaxeshead_kernel(tc, h, w_bytes, w_scale, g, u, emb, out):
+    nc = tc.nc
+    with ExitStack() as ctx:
+        keep = ctx.enter_context(tc.tile_pool(name="keep", bufs=1))
+        work = ctx.enter_context(tc.tile_pool(name="work", bufs=2))
+        lbank = ctx.enter_context(tc.psum_pool(name="lbank", bufs=5))
+        xbank = ctx.enter_context(tc.psum_pool(name="xbank", bufs=2))
+        zbank = ctx.enter_context(tc.psum_pool(name="zbank", bufs=1))
+
+        w_raw = keep.tile([P, K, T * D], U8, name="w_raw", align_bytes=64)
+        h_raw = keep.tile([P, NT, D], BF16, name="h_raw", align_bytes=64)
+        e_raw = keep.tile([P, NJ, T * D], BF16, name="e_raw", align_bytes=64)
+        scale = keep.tile([P, T], F32, name="scale")
+        g_sb = keep.tile([P, K, T], BF16, name="g_sb")
+        u_bf = keep.tile([P, K * T], BF16, name="u_bf")
+        u_sb = keep.tile([P, K * T], F32, name="u_sb")
+        ident = keep.tile([P, P], F32, name="ident")
+        one = keep.tile([P, 1], F32, name="one")
+
+        h_codes = keep.tile([P, N], U32, name="h_codes", align_bytes=64)
+        h_scales = keep.tile([P, N], U8, name="h_scales", align_bytes=64)
+        w_codes = keep.tile([P, K, D], U32, name="w_codes", align_bytes=64)
+        w_scales = keep.tile([P, K, D], U8, name="w_scales", align_bytes=64)
+        e_codes = keep.tile([P, V], U32, name="e_codes", align_bytes=64)
+        e_scales = keep.tile([P, V], U8, name="e_scales", align_bytes=64)
+        a_codes = keep.tile([P, UNITS, P], U32, name="a_codes", align_bytes=64)
+        a_scales = keep.tile([P, UNITS, P], U8, name="a_scales", align_bytes=64)
+        acc = keep.tile([P, NT, V], F32, name="acc")
+        z_ps = zbank.tile([P, UNITS], F32, name="z_ps")
+
+        w_view = w_bytes.rearrange("k (p j) e -> k p (j e)", j=T)
+        e_view = emb.rearrange("(j i p) d -> j p i d", i=4, p=P)
+
+        def load_w(k):
+            nc.sync.dma_start(out=w_raw[:, k, :], in_=w_view[k])
+
+        def load_e(j):
+            nc.sync.dma_start(out=e_raw[:, j, :].rearrange("p (i d) -> p i d", i=4), in_=e_view[j])
+
+        nc.sync.dma_start(out=scale[:], in_=w_scale.rearrange("o (p j) x -> p (o j x)", j=T))
+        load_w(0)
+        nc.sync.dma_start(out=h_raw[:], in_=h.rearrange("(p t) d -> p t d", t=NT))
+        load_e(0)
+        load_w(1)
+        load_e(1)
+        load_w(2)
+        load_e(2)
+        load_w(3)
+        load_e(3)
+        nc.vector.memset(one[:], 1.0)
+        nc.scalar.activation(out=one[:], in_=one[:], func=ACT.Exp)
+        make_identity(nc, ident[:])
+        nc.gpsimd.dma_start(out=g_sb[:], in_=g.rearrange("k (p t) -> p k t", t=T))
+        nc.gpsimd.dma_start(out=u_bf[:].rearrange("p (k t) -> p k t", t=T), in_=u.rearrange("k (p t) -> p k t", t=T))
+        nc.gpsimd.tensor_copy(out=u_sb[:], in_=u_bf[:])
+
+        wide = {}
+        grouped = {}
+
+        def widen(k, planes, on_scalar=True):
+            if k not in wide:
+                w_wide = work.tile([P, T, D], BF16, name="w_wide", align_bytes=64)
+                wide[k] = w_wide
+            for j in planes:
+                src = w_raw[:, k, j * D : (j + 1) * D].bitcast(FP8)
+                if on_scalar:
+                    nc.scalar.activation(out=wide[k][:, j, :], in_=src, func=ACT.Copy, scale=scale[:, j : j + 1])
+                else:
+                    nc.vector.tensor_scalar(out=wide[k][:, j, :], in0=src, scalar1=scale[:, j : j + 1], scalar2=None, op0=ALU.mult)
+
+        def interleave(k):
+            w_grouped = work.tile([P, D * T], BF16, name="w_grouped", align_bytes=64)
+            grouped[k] = w_grouped
+            dst = w_grouped[:].rearrange("p (t m j) -> p t m j", t=T, j=T)
+            src = wide[k][:].rearrange("p j (m t) -> p t m j", t=T)
+            if k in ():
+                nc.scalar.copy(out=dst, in_=src)
+            else:
+                nc.vector.tensor_copy(out=dst, in_=src)
+
+        def quant_w(k):
+            nc.vector.quantize_mx(out=w_codes[:, k, :].bitcast(FP8X4), scales=w_scales[:, k, :], in_=grouped[k][:])
+
+        def turn(words, dest):
+            for half in range(2):
+                bank = xbank.tile([P, 512], F32, name="bank")
+                for i in range(2):
+                    for v in range(2):
+                        row = 2 * half + i
+                        nc.tensor.transpose(
+                            bank[:, (2 * i + v) * P : (2 * i + v + 1) * P],
+                            words[:, 256 * row + v : 256 * (row + 1) : 2],
+                            ident[:],
+                        )
+                nc.scalar.copy(
+                    out=dest[:, half * 512 : (half + 1) * 512].rearrange("p (i r v) -> p i r v", i=2, v=2),
+                    in_=bank[:].rearrange("p (i v r) -> p i r v", i=2, v=2),
+                )
+
+        def turn_h():
+            h_grouped = keep.tile([P, N * T], BF16, name="h_grouped", align_bytes=64)
+            grouped["h"] = h_grouped
+            turn(h_raw[:].rearrange("p t d -> p (t d)").bitcast(F32), h_grouped[:].bitcast(F32))
+
+        def quant_h():
+            nc.vector.quantize_mx(out=h_codes[:].bitcast(FP8X4), scales=h_scales[:], in_=grouped["h"][:])
+
+        def turn_e(j):
+            e_grouped = work.tile([P, CH * T], BF16, name="e_grouped", align_bytes=64)
+            grouped["e", j] = e_grouped
+            turn(e_raw[:, j, :].bitcast(F32), e_grouped[:].bitcast(F32))
+
+        def quant_e(j):
+            cols = slice(j * CH, (j + 1) * CH)
+            nc.vector.quantize_mx(out=e_codes[:, cols].bitcast(FP8X4), scales=e_scales[:, cols], in_=grouped["e", j][:])
+
+        tvals = {}
+        avals = {}
+
+        def context(q):
+            if q >= UNITS:
+                return
+            nt, k = divmod(q, K)
+            rows = slice(nt * P, (nt + 1) * P)
+            bank = xbank.tile([P, 512], F32, name="bank")
+            for t in range(T):
+                cols = slice(t * P, (t + 1) * P)
+                nc.tensor.matmul_mx(
+                    out=bank[:, cols],
+                    lhsT=w_codes[:, k, cols].bitcast(FP8X4),
+                    lhsT_scale=w_scales[:, k, cols],
+                    rhs=h_codes[:, rows].bitcast(FP8X4),
+                    rhs_scale=h_scales[:, rows],
+                    start=True,
+                    stop=True,
+                )
+            t_sb = work.tile([P, P * T], F32, name="t_sb", bufs=4)
+            tvals[q] = t_sb
+            nc.scalar.activation(
+                out=t_sb[:].rearrange("p (n t) -> p n t", t=T),
+                in_=bank[:].rearrange("p (t n) -> p n t", t=T),
+                func=ACT.Tanh,
+            )
+
+        def gain(q):
+            if q >= UNITS:
+                return
+            k = q % K
+            a_bf = work.tile([P, P * T], BF16, name="a_bf", bufs=3, align_bytes=64)
+            avals[q] = a_bf
+            nc.vector.tensor_tensor(
+                out=a_bf[:].rearrange("p (n t) -> p n t", t=T),
+                in0=tvals[q][:].rearrange("p (n t) -> p n t", t=T),
+                in1=g_sb[:, k : k + 1, :].to_broadcast([P, P, T]),
+                op=ALU.mult,
+            )
+
+        def quant_a(q):
+            if q >= UNITS:
+                return
+            nc.vector.quantize_mx(out=a_codes[:, q, :].bitcast(FP8X4), scales=a_scales[:, q, :], in_=avals[q][:])
+
+        def mix_logit(q):
+            if q >= UNITS:
+                return
+            k = q % K
+            for t in range(T):
+                nc.tensor.matmul(
+                    z_ps[:, q : q + 1],
+                    lhsT=tvals[q][:, t : P * T : T],
+                    rhs=u_sb[:, k * T + t : k * T + t + 1],
+                    start=(t == 0),
+                    stop=(t == T - 1),
+                )
+
+        st = {}
+
+        def begin(nt):
+            e_sb = work.tile([P, K * NJ, CH], F32, name="e_sb", bufs=3)
+            negmax = work.tile([P, K * NJ], F32, name="negmax", bufs=4)
+            sums = work.tile([P, K * NJ], F32, name="sums", bufs=4)
+            low = work.tile([P, K], F32, name="low", bufs=4)
+            dif = work.tile([P, K * NJ], F32, name="dif", bufs=4)
+            fac = work.tile([P, K * NJ], F32, name="fac", bufs=4)
+            fsum = work.tile([P, K * NJ], F32, name="fsum", bufs=4)
+            tot = work.tile([P, K], F32, name="tot", bufs=4)
+            rec = work.tile([P, K], F32, name="rec", bufs=4)
+            pr = work.tile([P, K], F32, name="pr", bufs=4)
+            alpha = work.tile([P, K * NJ], F32, name="alpha", bufs=4)
+            st[nt] = dict(e=e_sb, negmax=negmax, sums=sums, low=low, dif=dif, fac=fac, fsum=fsum, tot=tot, rec=rec, pr=pr, alpha=alpha)
+
+        def step(q, j):
+            nt, k = divmod(q, K)
+            if k == 0 and j == 0:
+                begin(nt)
+            s = st[nt]
+            c = k * NJ + j
+            cols = slice(j * CH, (j + 1) * CH)
+            logits = lbank.tile([P, CH], F32, name="logits")
+            nc.tensor.matmul_mx(
+                out=logits[:],
+                lhsT=a_codes[:, q, :].bitcast(FP8X4),
+                lhsT_scale=a_scales[:, q, :],
+                rhs=e_codes[:, cols].bitcast(FP8X4),
+                rhs_scale=e_scales[:, cols],
+                start=True,
+                stop=True,
+            )
+            nc.vector.tensor_reduce(out=s["negmax"][:, c : c + 1], in_=logits[:], axis=AX.X, op=ALU.max, negate=True)
+            nc.scalar.activation(
+                out=s["e"][:, c, :],
+                in_=logits[:],
+                func=ACT.Exp,
+                bias=s["negmax"][:, c : c + 1],
+                accum_out=s["sums"][:, c : c + 1],
+            )
+
+        pis = {}
+
+        def pi_a(nt):
+            zneg = work.tile([P, 1], F32, name="zneg")
+            ez = work.tile([P, K], F32, name="ez")
+            zsum = work.tile([P, 1], F32, name="zsum")
+            pi = work.tile([P, K], F32, name="pi")
+            zcols = z_ps[:, nt * K : (nt + 1) * K]
+            nc.vector.tensor_reduce(out=zneg[:], in_=zcols, axis=AX.X, op=ALU.max, negate=True)
+            nc.scalar.activation(out=ez[:], in_=zcols, func=ACT.Exp, bias=zneg[:], accum_out=zsum[:])
+            pis[nt] = (ez, zsum, pi)
+
+        def pi_b(nt):
+            ez, zsum, pi = pis[nt]
+            zrec = work.tile([P, 1], F32, name="zrec")
+            nc.vector.reciprocal(out=zrec[:], in_=zsum[:])
+            nc.vector.tensor_scalar(out=pi[:], in0=ez[:], scalar1=zrec[:], scalar2=None, op0=ALU.mult)
+
+        def cube(tile, k0, k1):
+            return tile[:, k0 * NJ : k1 * NJ].rearrange("p (k j) -> p k j", j=NJ)
+
+        def chain_a(nt, k0, k1):
+            s = st[nt]
+            nc.vector.tensor_reduce(out=s["low"][:, k0:k1], in_=cube(s["negmax"], k0, k1), axis=AX.X, op=ALU.min)
+            nc.vector.tensor_tensor(
+                out=cube(s["dif"], k0, k1),
+                in0=s["low"][:, k0:k1].unsqueeze(2).to_broadcast([P, k1 - k0, NJ]),
+                in1=cube(s["negmax"], k0, k1),
+                op=ALU.subtract,
+            )
+            nc.scalar.activation(out=s["fac"][:, k0 * NJ : k1 * NJ], in_=s["dif"][:, k0 * NJ : k1 * NJ], func=ACT.Exp)
+
+        def chain_b(nt, k0, k1):
+            s = st[nt]
+            pi = pis[nt][2]
+            cols = slice(k0 * NJ, k1 * NJ)
+            nc.vector.tensor_tensor(out=s["fsum"][:, cols], in0=s["fac"][:, cols], in1=s["sums"][:, cols], op=ALU.mult)
+            nc.vector.tensor_reduce(out=s["tot"][:, k0:k1], in_=cube(s["fsum"], k0, k1), axis=AX.X, op=ALU.add)
+            nc.vector.reciprocal(out=s["rec"][:, k0:k1], in_=s["tot"][:, k0:k1])
+            nc.vector.tensor_tensor(out=s["pr"][:, k0:k1], in0=s["rec"][:, k0:k1], in1=pi[:, k0:k1], op=ALU.mult)
+            nc.vector.tensor_tensor(
+                out=cube(s["alpha"], k0, k1),
+                in0=cube(s["fac"], k0, k1),
+                in1=s["pr"][:, k0:k1].unsqueeze(2).to_broadcast([P, k1 - k0, NJ]),
+                op=ALU.mult,
+            )
+
+        diags = {}
+        sums_ps = {}
+
+        def build_diag(nt, j, ks):
+            for k in ks:
+                c = k * NJ + j
+                diag = work.tile([P, P], F32, name="diag", bufs=12)
+                diags[nt, c] = diag
+                nc.gpsimd.tensor_scalar(
+                    out=diag[:], in0=ident[:], scalar1=st[nt]["alpha"][:, c : c + 1], scalar2=0.0, op0=ALU.mult, op1=ALU.add
+                )
+
+        def mix(nt, j, k):
+            m = ON_PE[nt][j]
+            c = k * NJ + j
+            cols = slice(j * CH, (j + 1) * CH)
+            e = st[nt]["e"][:, c, :]
+            weight = st[nt]["alpha"][:, c : c + 1]
+            dst = acc[:, nt, cols]
+            if k < m:
+                if k == 0:
+                    bank = xbank.tile([P, 512], F32, name="bank")
+                    sums_ps[nt, j] = bank
+                nc.tensor.matmul(sums_ps[nt, j][:], lhsT=diags[nt, c][:], rhs=e, start=(k == 0), stop=(k == m - 1))
+            elif k == 0:
+                nc.scalar.activation(out=dst, in_=e, func=ACT.Copy, scale=weight)
+            else:
+                nc.vector.scalar_tensor_tensor(
+                    out=dst, in0=e, scalar=weight, in1=sums_ps[nt, j][:] if k == m else dst, op0=ALU.mult, op1=ALU.add
+                )
+
+        plan = {}
+
+        def at(q, j, fn, *args):
+            plan.setdefault((q, j), []).append((fn, args))
+
+        widen(0, (0, 1))
+        widen(0, (2, 3), False)
+        turn_h()
+        interleave(0)
+        quant_w(0)
+        turn_e(0)
+        quant_h()
+        context(0)
+        quant_e(0)
+        widen(1, (0, 1, 2, 3))
+        gain(0)
+        interleave(1)
+        quant_a(0)
+        turn_e(1)
+
+        at(0, 0, quant_w, 1)
+        at(0, 0, quant_e, 1)
+        at(0, 0, context, 1)
+        at(0, 0, turn_e, 2)
+        at(0, 1, quant_e, 2)
+        at(0, 1, gain, 1)
+        at(0, 1, widen, 2, (0, 1))
+        at(0, 1, turn_e, 3)
+        at(0, 2, quant_e, 3)
+        at(0, 2, quant_a, 1)
+        at(0, 2, widen, 2, (2, 3))
+        at(0, 3, interleave, 2)
+        at(0, 3, mix_logit, 0)
+        at(1, 0, quant_w, 2)
+        at(1, 0, context, 2)
+        at(1, 0, widen, 3, (0, 1))
+        at(1, 1, widen, 3, (2, 3))
+        at(1, 2, mix_logit, 1)
+        at(1, 3, gain, 2)
+        at(1, 3, interleave, 3)
+        at(1, 3, quant_a, 2)
+        at(2, 0, quant_w, 3)
+        at(2, 0, context, 3)
+        at(2, 1, context, 4)
+        at(2, 1, mix_logit, 2)
+        at(2, 2, gain, 3)
+        at(2, 3, context, 5)
+        at(2, 3, gain, 4)
+        at(2, 3, quant_a, 3)
+        at(3, 0, quant_a, 4)
+        at(3, 0, mix_logit, 3)
+        at(3, 1, gain, 5)
+        at(3, 2, context, 6)
+        at(3, 2, mix_logit, 4)
+        at(3, 3, quant_a, 5)
+        at(3, 3, mix_logit, 5)
+        for q in range(4, UNITS):
+            at(q, 0, gain, q + 2)
+            at(q, 0, context, q + 3)
+            at(q, 2, quant_a, q + 2)
+            at(q, 3, mix_logit, q + 2)
+        for nt in range(NT):
+            at(nt * K + 3, 1, pi_a, nt)
+            at(nt * K + 3, 3, pi_b, nt)
+        for nt in range(NT - 1):
+            base = (nt + 1) * K
+            at(base, 0, chain_a, nt, 0, K)
+            at(base + 1, 0, chain_b, nt, 0, K)
+            for j in range(NJ):
+                at(base + 1, 0, build_diag, nt, j, range(ON_PE[nt][j]))
+                for k in range(K):
+                    when = base * NJ + LAG + 3 * j + k
+                    at(when // NJ, when % NJ, mix, nt, j, k)
+        last = NT - 1
+        at(UNITS - 1, 0, chain_a, last, 0, K - 1)
+
+        def run(q, j):
+            for fn, args in plan.get((q, j), ()):
+                fn(*args)
+
+        for q in range(UNITS):
+            for j in range(NJ):
+                step(q, j)
+                run(q, j)
+        chain_a(last, K - 1, K)
+        chain_b(last, 0, K - 1)
+        for j in range(NJ):
+            build_diag(last, j, range(ON_PE[last][j]))
+        for extra in range(8):
+            run(UNITS + extra // NJ, extra % NJ)
+        vocab = keep.tile([P, 1], F32, name="vocab")
+        nc.vector.tensor_scalar(out=vocab[:], in0=st[last]["fac"][:, K * NJ - 1 : K * NJ], scalar1=0.0, scalar2=float(V), op0=ALU.mult, op1=ALU.add)
+        for nt in range(NT - 1):
+            nc.scalar.activation(out=acc[:, nt, :], in_=acc[:, nt, :], func=ACT.Ln, scale=vocab[:])
+        for j in range(NJ):
+            for k in range(K - 1):
+                mix(last, j, k)
+        chain_b(last, K - 1, K)
+        out_view = out.rearrange("(p t) v -> t p v", t=NT)
+        for nt in range(NT - 1):
+            nc.sync.dma_start(out=out_view[nt], in_=acc[:, nt, :])
+        for j in range(NJ):
+            cols = slice(j * CH, (j + 1) * CH)
+            mix(last, j, K - 1)
+            nc.scalar.activation(out=acc[:, last, cols], in_=acc[:, last, cols], func=ACT.Ln, scale=vocab[:])
+            nc.sync.dma_start(out=out_view[last][:, cols], in_=acc[:, last, cols])

@@ -39,9 +39,9 @@ def tile_mixtureofsoftmaxeshead_kernel(tc, h, w_bytes, w_scale, g, u, emb, out):
         h_raw = keep.tile([P, NT, D], BF16, name="h_raw", align_bytes=64)
         e_raw = keep.tile([P, NJ, T * D], BF16, name="e_raw", align_bytes=64)
         scale = keep.tile([P, T], F32, name="scale")
-        g_sb = keep.tile([P, K, T], BF16, name="g_sb")
-        u_bf = keep.tile([P, K * T], BF16, name="u_bf")
-        u_sb = keep.tile([P, K * T], F32, name="u_sb")
+        gu_raw = keep.tile([P, D], BF16, name="gu_raw", align_bytes=64)
+        gu_sb = keep.tile([P, 2 * K * T], BF16, name="gu_sb", align_bytes=64)
+        u_sb = keep.tile([P, T * K], F32, name="u_sb")
         ident = keep.tile([P, P], F32, name="ident")
         one = keep.tile([P, 1], F32, name="one")
 
@@ -54,7 +54,7 @@ def tile_mixtureofsoftmaxeshead_kernel(tc, h, w_bytes, w_scale, g, u, emb, out):
         a_codes = keep.tile([P, UNITS, P], U32, name="a_codes", align_bytes=64)
         a_scales = keep.tile([P, UNITS, P], U8, name="a_scales", align_bytes=64)
         acc = keep.tile([P, NT, V], F32, name="acc")
-        z_ps = zbank.tile([P, UNITS], F32, name="z_ps")
+        z_ps = zbank.tile([P, UNITS * K], F32, name="z_ps")
 
         w_view = w_bytes.rearrange("k (p j) e -> k p (j e)", j=T)
         e_view = emb.rearrange("(j i p) d -> j p i d", i=4, p=P)
@@ -65,8 +65,11 @@ def tile_mixtureofsoftmaxeshead_kernel(tc, h, w_bytes, w_scale, g, u, emb, out):
         def load_e(j):
             nc.sync.dma_start(out=e_raw[:, j, :].rearrange("p (i d) -> p i d", i=4), in_=e_view[j])
 
+        nc.vector.memset(gu_raw[:].bitcast(U32), 0)
         nc.sync.dma_start(out=scale[:], in_=w_scale.rearrange("o (p j) x -> p (o j x)", j=T))
         load_w(0)
+        nc.sync.dma_start(out=gu_raw[0:K, :], in_=g)
+        nc.sync.dma_start(out=gu_raw[K : 2 * K, :], in_=u)
         nc.sync.dma_start(out=h_raw[:], in_=h.rearrange("(p t) d -> p t d", t=NT))
         load_e(0)
         load_w(1)
@@ -78,9 +81,6 @@ def tile_mixtureofsoftmaxeshead_kernel(tc, h, w_bytes, w_scale, g, u, emb, out):
         nc.vector.memset(one[:], 1.0)
         nc.scalar.activation(out=one[:], in_=one[:], func=ACT.Exp)
         make_identity(nc, ident[:])
-        nc.gpsimd.dma_start(out=g_sb[:], in_=g.rearrange("k (p t) -> p k t", t=T))
-        nc.gpsimd.dma_start(out=u_bf[:].rearrange("p (k t) -> p k t", t=T), in_=u.rearrange("k (p t) -> p k t", t=T))
-        nc.gpsimd.tensor_copy(out=u_sb[:], in_=u_bf[:])
 
         wide = {}
         grouped = {}
@@ -125,6 +125,20 @@ def tile_mixtureofsoftmaxeshead_kernel(tc, h, w_bytes, w_scale, g, u, emb, out):
                     in_=bank[:].rearrange("p (i v r) -> p i r v", i=2, v=2),
                 )
 
+        def turn_gu():
+            bank = xbank.tile([P, 512], F32, name="bank")
+            words = gu_raw[:].bitcast(F32)
+            for v in range(2):
+                nc.tensor.transpose(bank[:, v * P : (v + 1) * P], words[:, v : 2 * P : 2], ident[:])
+            nc.vector.tensor_copy(
+                out=gu_sb[:].bitcast(F32).rearrange("p (r v) -> p r v", v=2),
+                in_=bank[:, 0 : 2 * P].rearrange("p (v r) -> p r v", v=2)[:, 0 : 2 * K, :],
+            )
+            nc.vector.tensor_copy(
+                out=u_sb[:].rearrange("p (t k) -> p t k", k=K),
+                in_=gu_sb[:, K * T : 2 * K * T].rearrange("p (k t) -> p t k", t=T),
+            )
+
         def turn_h():
             h_grouped = keep.tile([P, N * T], BF16, name="h_grouped", align_bytes=64)
             grouped["h"] = h_grouped
@@ -165,8 +179,8 @@ def tile_mixtureofsoftmaxeshead_kernel(tc, h, w_bytes, w_scale, g, u, emb, out):
             t_sb = work.tile([P, P * T], F32, name="t_sb", bufs=4)
             tvals[q] = t_sb
             nc.scalar.activation(
-                out=t_sb[:].rearrange("p (n t) -> p n t", t=T),
-                in_=bank[:].rearrange("p (t n) -> p n t", t=T),
+                out=t_sb[:],
+                in_=bank[:],
                 func=ACT.Tanh,
             )
 
@@ -178,8 +192,8 @@ def tile_mixtureofsoftmaxeshead_kernel(tc, h, w_bytes, w_scale, g, u, emb, out):
             avals[q] = a_bf
             nc.vector.tensor_tensor(
                 out=a_bf[:].rearrange("p (n t) -> p n t", t=T),
-                in0=tvals[q][:].rearrange("p (n t) -> p n t", t=T),
-                in1=g_sb[:, k : k + 1, :].to_broadcast([P, P, T]),
+                in0=tvals[q][:].rearrange("p (t n) -> p n t", t=T),
+                in1=gu_sb[:, k * T : (k + 1) * T].unsqueeze(1).to_broadcast([P, P, T]),
                 op=ALU.mult,
             )
 
@@ -191,12 +205,11 @@ def tile_mixtureofsoftmaxeshead_kernel(tc, h, w_bytes, w_scale, g, u, emb, out):
         def mix_logit(q):
             if q >= UNITS:
                 return
-            k = q % K
             for t in range(T):
                 nc.tensor.matmul(
-                    z_ps[:, q : q + 1],
-                    lhsT=tvals[q][:, t : P * T : T],
-                    rhs=u_sb[:, k * T + t : k * T + t + 1],
+                    z_ps[:, q * K : (q + 1) * K],
+                    lhsT=tvals[q][:, t * P : (t + 1) * P],
+                    rhs=u_sb[:, t * K : (t + 1) * K],
                     start=(t == 0),
                     stop=(t == T - 1),
                 )
@@ -250,7 +263,7 @@ def tile_mixtureofsoftmaxeshead_kernel(tc, h, w_bytes, w_scale, g, u, emb, out):
             ez = work.tile([P, K], F32, name="ez")
             zsum = work.tile([P, 1], F32, name="zsum")
             pi = work.tile([P, K], F32, name="pi")
-            zcols = z_ps[:, nt * K : (nt + 1) * K]
+            zcols = z_ps[:, nt * K * K : (nt + 1) * K * K : K + 1]
             nc.vector.tensor_reduce(out=zneg[:], in_=zcols, axis=AX.X, op=ALU.max, negate=True)
             nc.scalar.activation(out=ez[:], in_=zcols, func=ACT.Exp, bias=zneg[:], accum_out=zsum[:])
             pis[nt] = (ez, zsum, pi)
@@ -328,6 +341,7 @@ def tile_mixtureofsoftmaxeshead_kernel(tc, h, w_bytes, w_scale, g, u, emb, out):
 
         widen(0, (0, 1))
         widen(0, (2, 3), False)
+        turn_gu()
         turn_h()
         interleave(0)
         quant_w(0)

@@ -23,7 +23,8 @@ CH = 512
 NJ = V // CH
 UNITS = NT * K
 ON_PE = ((3, 0, 3, 0), (3, 0, 3, 0), (3, 0, 3, 0), (1, 1, 1, 1))
-LAG = 9
+SHARED = 1
+LAG = 11
 
 
 def tile_mixtureofsoftmaxeshead_kernel(tc, h, w_bytes, w_scale, g, u, emb, out):
@@ -51,8 +52,8 @@ def tile_mixtureofsoftmaxeshead_kernel(tc, h, w_bytes, w_scale, g, u, emb, out):
         w_scales = keep.tile([P, K, D], U8, name="w_scales", align_bytes=64)
         e_codes = keep.tile([P, V], U32, name="e_codes", align_bytes=64)
         e_scales = keep.tile([P, V], U8, name="e_scales", align_bytes=64)
-        a_codes = keep.tile([P, UNITS, P], U32, name="a_codes", align_bytes=64)
-        a_scales = keep.tile([P, UNITS, P], U8, name="a_scales", align_bytes=64)
+        a_codes = keep.tile([P, UNITS * P], U32, name="a_codes", align_bytes=64)
+        a_scales = keep.tile([P, UNITS * P], U8, name="a_scales", align_bytes=64)
         acc = keep.tile([P, NT, V], F32, name="acc")
         z_ps = zbank.tile([P, UNITS * K], F32, name="z_ps")
 
@@ -109,7 +110,7 @@ def tile_mixtureofsoftmaxeshead_kernel(tc, h, w_bytes, w_scale, g, u, emb, out):
         def quant_w(k):
             nc.vector.quantize_mx(out=w_codes[:, k, :].bitcast(FP8X4), scales=w_scales[:, k, :], in_=grouped[k][:])
 
-        def turn(words, dest):
+        def turn(words, dest, shared=False):
             for half in range(2):
                 bank = xbank.tile([P, 512], F32, name="bank")
                 for i in range(2):
@@ -120,10 +121,12 @@ def tile_mixtureofsoftmaxeshead_kernel(tc, h, w_bytes, w_scale, g, u, emb, out):
                             words[:, 256 * row + v : 256 * (row + 1) : 2],
                             ident[:],
                         )
-                nc.scalar.copy(
-                    out=dest[:, half * 512 : (half + 1) * 512].rearrange("p (i r v) -> p i r v", i=2, v=2),
-                    in_=bank[:].rearrange("p (i v r) -> p i r v", i=2, v=2),
-                )
+                out_words = dest[:, half * 512 : (half + 1) * 512].rearrange("p (i r v) -> p i r v", i=2, v=2)
+                in_words = bank[:].rearrange("p (i v r) -> p i r v", i=2, v=2)
+                if shared and half == 1:
+                    nc.vector.tensor_copy(out=out_words, in_=in_words)
+                else:
+                    nc.scalar.copy(out=out_words, in_=in_words)
 
         def turn_gu():
             bank = xbank.tile([P, 512], F32, name="bank")
@@ -142,7 +145,7 @@ def tile_mixtureofsoftmaxeshead_kernel(tc, h, w_bytes, w_scale, g, u, emb, out):
         def turn_h():
             h_grouped = keep.tile([P, N * T], BF16, name="h_grouped", align_bytes=64)
             grouped["h"] = h_grouped
-            turn(h_raw[:].rearrange("p t d -> p (t d)").bitcast(F32), h_grouped[:].bitcast(F32))
+            turn(h_raw[:].rearrange("p t d -> p (t d)").bitcast(F32), h_grouped[:].bitcast(F32), True)
 
         def quant_h():
             nc.vector.quantize_mx(out=h_codes[:].bitcast(FP8X4), scales=h_scales[:], in_=grouped["h"][:])
@@ -150,7 +153,7 @@ def tile_mixtureofsoftmaxeshead_kernel(tc, h, w_bytes, w_scale, g, u, emb, out):
         def turn_e(j):
             e_grouped = work.tile([P, CH * T], BF16, name="e_grouped", align_bytes=64)
             grouped["e", j] = e_grouped
-            turn(e_raw[:, j, :].bitcast(F32), e_grouped[:].bitcast(F32))
+            turn(e_raw[:, j, :].bitcast(F32), e_grouped[:].bitcast(F32), j < SHARED)
 
         def quant_e(j):
             cols = slice(j * CH, (j + 1) * CH)
@@ -188,10 +191,12 @@ def tile_mixtureofsoftmaxeshead_kernel(tc, h, w_bytes, w_scale, g, u, emb, out):
             if q >= UNITS:
                 return
             k = q % K
-            a_bf = work.tile([P, P * T], BF16, name="a_bf", bufs=3, align_bytes=64)
-            avals[q] = a_bf
+            if q % 2 == 0:
+                a_pair = work.tile([P, 2 * P * T], BF16, name="a_pair", bufs=2, align_bytes=64)
+                avals[q // 2] = a_pair
+            a_bf = avals[q // 2][:, (q % 2) * P * T : (q % 2 + 1) * P * T]
             nc.vector.tensor_tensor(
-                out=a_bf[:].rearrange("p (n t) -> p n t", t=T),
+                out=a_bf.rearrange("p (n t) -> p n t", t=T),
                 in0=tvals[q][:].rearrange("p (t n) -> p n t", t=T),
                 in1=gu_sb[:, k * T : (k + 1) * T].unsqueeze(1).to_broadcast([P, P, T]),
                 op=ALU.mult,
@@ -200,7 +205,12 @@ def tile_mixtureofsoftmaxeshead_kernel(tc, h, w_bytes, w_scale, g, u, emb, out):
         def quant_a(q):
             if q >= UNITS:
                 return
-            nc.vector.quantize_mx(out=a_codes[:, q, :].bitcast(FP8X4), scales=a_scales[:, q, :], in_=avals[q][:])
+            count = 1 if q < K else 2
+            if q >= K and q % 2 == 0:
+                return
+            words = slice((q + 1 - count) * P, (q + 1) * P)
+            a_bf = avals[q // 2][:, (q % 2 + 1 - count) * P * T : (q % 2 + 1) * P * T]
+            nc.vector.quantize_mx(out=a_codes[:, words].bitcast(FP8X4), scales=a_scales[:, words], in_=a_bf)
 
         def mix_logit(q):
             if q >= UNITS:
@@ -240,8 +250,8 @@ def tile_mixtureofsoftmaxeshead_kernel(tc, h, w_bytes, w_scale, g, u, emb, out):
             logits = lbank.tile([P, CH], F32, name="logits")
             nc.tensor.matmul_mx(
                 out=logits[:],
-                lhsT=a_codes[:, q, :].bitcast(FP8X4),
-                lhsT_scale=a_scales[:, q, :],
+                lhsT=a_codes[:, q * P : (q + 1) * P].bitcast(FP8X4),
+                lhsT_scale=a_scales[:, q * P : (q + 1) * P],
                 rhs=e_codes[:, cols].bitcast(FP8X4),
                 rhs_scale=e_scales[:, cols],
                 start=True,
@@ -327,6 +337,8 @@ def tile_mixtureofsoftmaxeshead_kernel(tc, h, w_bytes, w_scale, g, u, emb, out):
                     bank = xbank.tile([P, 512], F32, name="bank")
                     sums_ps[nt, j] = bank
                 nc.tensor.matmul(sums_ps[nt, j][:], lhsT=diags[nt, c][:], rhs=e, start=(k == 0), stop=(k == m - 1))
+                if k == K - 1:
+                    nc.scalar.copy(out=dst, in_=sums_ps[nt, j][:])
             elif k == 0:
                 nc.scalar.activation(out=dst, in_=e, func=ACT.Copy, scale=weight)
             else:
@@ -341,8 +353,8 @@ def tile_mixtureofsoftmaxeshead_kernel(tc, h, w_bytes, w_scale, g, u, emb, out):
 
         widen(0, (0, 1))
         widen(0, (2, 3), False)
-        turn_gu()
         turn_h()
+        turn_gu()
         interleave(0)
         quant_w(0)
         turn_e(0)
@@ -391,11 +403,14 @@ def tile_mixtureofsoftmaxeshead_kernel(tc, h, w_bytes, w_scale, g, u, emb, out):
         at(3, 2, mix_logit, 4)
         at(3, 3, quant_a, 5)
         at(3, 3, mix_logit, 5)
+        at(3, 3, gain, 6)
+        at(3, 3, context, 7)
+        at(3, 3, mix_logit, 6)
         for q in range(4, UNITS):
-            at(q, 0, gain, q + 2)
-            at(q, 0, context, q + 3)
-            at(q, 2, quant_a, q + 2)
-            at(q, 3, mix_logit, q + 2)
+            at(q, 0, gain, q + 3)
+            at(q, 0, context, q + 4)
+            at(q, 2, quant_a, q + 3)
+            at(q, 3, mix_logit, q + 3)
         for nt in range(NT):
             at(nt * K + 3, 1, pi_a, nt)
             at(nt * K + 3, 3, pi_b, nt)
@@ -423,7 +438,7 @@ def tile_mixtureofsoftmaxeshead_kernel(tc, h, w_bytes, w_scale, g, u, emb, out):
         chain_b(last, 0, K - 1)
         for j in range(NJ):
             build_diag(last, j, range(ON_PE[last][j]))
-        for extra in range(8):
+        for extra in range(16):
             run(UNITS + extra // NJ, extra % NJ)
         vocab = keep.tile([P, 1], F32, name="vocab")
         nc.vector.tensor_scalar(out=vocab[:], in0=st[last]["fac"][:, K * NJ - 1 : K * NJ], scalar1=0.0, scalar2=float(V), op0=ALU.mult, op1=ALU.add)

from contextlib import ExitStack

import concourse.mybir as mybir
from concourse.masks import make_identity

N, D, K, V = 512, 512, 4, 2048
FLOPS = 2 * N * D * K * D + 2 * N * K * D * V

F32 = mybir.dt.float32
BF16 = mybir.dt.bfloat16
U32 = mybir.dt.uint32
U8 = mybir.dt.uint8
FP8 = mybir.dt.float8_e4m3fn
FP8X4 = mybir.dt.float8_e4m3fn_x4
ACT = mybir.ActivationFunctionType
ALU = mybir.AluOpType
AX = mybir.AxisListType

P = 128
T = 4
NT = N // P
CH = 512
NJ = V // CH
UNITS = NT * K
ON_PE = ((3, 0, 3, 0), (3, 0, 3, 0), (3, 0, 3, 0), (1, 1, 1, 1))
SHARED = 1
LAG = 11


def tile_mixtureofsoftmaxeshead_kernel(tc, h, w_bytes, w_scale, g, u, emb, out):
    nc = tc.nc
    with ExitStack() as ctx:
        keep = ctx.enter_context(tc.tile_pool(name="keep", bufs=1))
        work = ctx.enter_context(tc.tile_pool(name="work", bufs=2))
        lbank = ctx.enter_context(tc.psum_pool(name="lbank", bufs=5))
        xbank = ctx.enter_context(tc.psum_pool(name="xbank", bufs=2))
        zbank = ctx.enter_context(tc.psum_pool(name="zbank", bufs=1))

        w_raw = keep.tile([P, K, T * D], U8, name="w_raw", align_bytes=64)
        h_raw = keep.tile([P, NT, D], BF16, name="h_raw", align_bytes=64)
        e_raw = keep.tile([P, NJ, T * D], BF16, name="e_raw", align_bytes=64)
        scale = keep.tile([P, T], F32, name="scale")
        gu_raw = keep.tile([P, D], BF16, name="gu_raw", align_bytes=64)
        gu_sb = keep.tile([P, 2 * K * T], BF16, name="gu_sb", align_bytes=64)
        u_sb = keep.tile([P, T * K], F32, name="u_sb")
        ident = keep.tile([P, P], F32, name="ident")
        one = keep.tile([P, 1], F32, name="one")

        h_codes = keep.tile([P, N], U32, name="h_codes", align_bytes=64)
        h_scales = keep.tile([P, N], U8, name="h_scales", align_bytes=64)
        w_codes = keep.tile([P, K, D], U32, name="w_codes", align_bytes=64)
        w_scales = keep.tile([P, K, D], U8, name="w_scales", align_bytes=64)
        e_codes = keep.tile([P, V], U32, name="e_codes", align_bytes=64)
        e_scales = keep.tile([P, V], U8, name="e_scales", align_bytes=64)
        a_codes = keep.tile([P, UNITS * P], U32, name="a_codes", align_bytes=64)
        a_scales = keep.tile([P, UNITS * P], U8, name="a_scales", align_bytes=64)
        acc = keep.tile([P, NT, V], F32, name="acc")
        z_ps = zbank.tile([P, UNITS * K], F32, name="z_ps")

        w_view = w_bytes.rearrange("k (p j) e -> k p (j e)", j=T)
        e_view = emb.rearrange("(j i p) d -> j p i d", i=4, p=P)

        def load_w(k):
            nc.sync.dma_start(out=w_raw[:, k, :], in_=w_view[k])

        def load_e(j):
            nc.sync.dma_start(out=e_raw[:, j, :].rearrange("p (i d) -> p i d", i=4), in_=e_view[j])

        nc.vector.memset(gu_raw[:].bitcast(U32), 0)
        nc.sync.dma_start(out=scale[:], in_=w_scale.rearrange("o (p j) x -> p (o j x)", j=T))
        load_w(0)
        nc.sync.dma_start(out=gu_raw[0:K, :], in_=g)
        nc.sync.dma_start(out=gu_raw[K : 2 * K, :], in_=u)
        nc.sync.dma_start(out=h_raw[:], in_=h.rearrange("(p t) d -> p t d", t=NT))
        load_e(0)
        load_w(1)
        load_e(1)
        load_w(2)
        load_e(2)
        load_w(3)
        load_e(3)
        nc.vector.memset(one[:], 1.0)
        nc.scalar.activation(out=one[:], in_=one[:], func=ACT.Exp)
        make_identity(nc, ident[:])

        wide = {}
        grouped = {}

        def widen(k, planes, on_scalar=True):
            if k not in wide:
                w_wide = work.tile([P, T, D], BF16, name="w_wide", align_bytes=64)
                wide[k] = w_wide
            for j in planes:
                src = w_raw[:, k, j * D : (j + 1) * D].bitcast(FP8)
                if on_scalar:
                    nc.scalar.activation(out=wide[k][:, j, :], in_=src, func=ACT.Copy, scale=scale[:, j : j + 1])
                else:
                    nc.vector.tensor_scalar(out=wide[k][:, j, :], in0=src, scalar1=scale[:, j : j + 1], scalar2=None, op0=ALU.mult)

        def interleave(k):
            w_grouped = work.tile([P, D * T], BF16, name="w_grouped", align_bytes=64)
            grouped[k] = w_grouped
            dst = w_grouped[:].rearrange("p (t m j) -> p t m j", t=T, j=T)
            src = wide[k][:].rearrange("p j (m t) -> p t m j", t=T)
            if k in ():
                nc.scalar.copy(out=dst, in_=src)
            else:
                nc.vector.tensor_copy(out=dst, in_=src)

        def quant_w(k):
            nc.vector.quantize_mx(out=w_codes[:, k, :].bitcast(FP8X4), scales=w_scales[:, k, :], in_=grouped[k][:])

        def turn(words, dest, shared=False):
            for half in range(2):
                bank = xbank.tile([P, 512], F32, name="bank")
                for i in range(2):
                    for v in range(2):
                        row = 2 * half + i
                        nc.tensor.transpose(
                            bank[:, (2 * i + v) * P : (2 * i + v + 1) * P],
                            words[:, 256 * row + v : 256 * (row + 1) : 2],
                            ident[:],
                        )
                out_words = dest[:, half * 512 : (half + 1) * 512].rearrange("p (i r v) -> p i r v", i=2, v=2)
                in_words = bank[:].rearrange("p (i v r) -> p i r v", i=2, v=2)
                if shared and half == 1:
                    nc.vector.tensor_copy(out=out_words, in_=in_words)
                else:
                    nc.scalar.copy(out=out_words, in_=in_words)

        def turn_gu():
            bank = xbank.tile([P, 512], F32, name="bank")
            words = gu_raw[:].bitcast(F32)
            for v in range(2):
                nc.tensor.transpose(bank[:, v * P : (v + 1) * P], words[:, v : 2 * P : 2], ident[:])
            nc.vector.tensor_copy(
                out=gu_sb[:].bitcast(F32).rearrange("p (r v) -> p r v", v=2),
                in_=bank[:, 0 : 2 * P].rearrange("p (v r) -> p r v", v=2)[:, 0 : 2 * K, :],
            )
            nc.vector.tensor_copy(
                out=u_sb[:].rearrange("p (t k) -> p t k", k=K),
                in_=gu_sb[:, K * T : 2 * K * T].rearrange("p (k t) -> p t k", t=T),
            )

        def turn_h():
            h_grouped = keep.tile([P, N * T], BF16, name="h_grouped", align_bytes=64)
            grouped["h"] = h_grouped
            turn(h_raw[:].rearrange("p t d -> p (t d)").bitcast(F32), h_grouped[:].bitcast(F32), True)

        def quant_h():
            nc.vector.quantize_mx(out=h_codes[:].bitcast(FP8X4), scales=h_scales[:], in_=grouped["h"][:])

        def turn_e(j):
            e_grouped = work.tile([P, CH * T], BF16, name="e_grouped", align_bytes=64)
            grouped["e", j] = e_grouped
            turn(e_raw[:, j, :].bitcast(F32), e_grouped[:].bitcast(F32), j < SHARED)

        def quant_e(j):
            cols = slice(j * CH, (j + 1) * CH)
            nc.vector.quantize_mx(out=e_codes[:, cols].bitcast(FP8X4), scales=e_scales[:, cols], in_=grouped["e", j][:])

        tvals = {}
        avals = {}

        def context(q):
            if q >= UNITS:
                return
            nt, k = divmod(q, K)
            rows = slice(nt * P, (nt + 1) * P)
            bank = xbank.tile([P, 512], F32, name="bank")
            for t in range(T):
                cols = slice(t * P, (t + 1) * P)
                nc.tensor.matmul_mx(
                    out=bank[:, cols],
                    lhsT=w_codes[:, k, cols].bitcast(FP8X4),
                    lhsT_scale=w_scales[:, k, cols],
                    rhs=h_codes[:, rows].bitcast(FP8X4),
                    rhs_scale=h_scales[:, rows],
                    start=True,
                    stop=True,
                )
            t_sb = work.tile([P, P * T], F32, name="t_sb", bufs=4)
            tvals[q] = t_sb
            nc.scalar.activation(
                out=t_sb[:],
                in_=bank[:],
                func=ACT.Tanh,
            )

        def gain(q):
            if q >= UNITS:
                return
            k = q % K
            if q % 2 == 0:
                a_pair = work.tile([P, 2 * P * T], BF16, name="a_pair", bufs=2, align_bytes=64)
                avals[q // 2] = a_pair
            a_bf = avals[q // 2][:, (q % 2) * P * T : (q % 2 + 1) * P * T]
            nc.vector.tensor_tensor(
                out=a_bf.rearrange("p (n t) -> p n t", t=T),
                in0=tvals[q][:].rearrange("p (t n) -> p n t", t=T),
                in1=gu_sb[:, k * T : (k + 1) * T].unsqueeze(1).to_broadcast([P, P, T]),
                op=ALU.mult,
            )

        def quant_a(q):
            if q >= UNITS:
                return
            count = 1 if q < K else 2
            if q >= K and q % 2 == 0:
                return
            words = slice((q + 1 - count) * P, (q + 1) * P)
            a_bf = avals[q // 2][:, (q % 2 + 1 - count) * P * T : (q % 2 + 1) * P * T]
            nc.vector.quantize_mx(out=a_codes[:, words].bitcast(FP8X4), scales=a_scales[:, words], in_=a_bf)

        def mix_logit(q):
            if q >= UNITS:
                return
            for t in range(T):
                nc.tensor.matmul(
                    z_ps[:, q * K : (q + 1) * K],
                    lhsT=tvals[q][:, t * P : (t + 1) * P],
                    rhs=u_sb[:, t * K : (t + 1) * K],
                    start=(t == 0),
                    stop=(t == T - 1),
                )

        st = {}

        def begin(nt):
            e_sb = work.tile([P, K * NJ, CH], F32, name="e_sb", bufs=3)
            negmax = work.tile([P, K * NJ], F32, name="negmax", bufs=4)
            sums = work.tile([P, K * NJ], F32, name="sums", bufs=4)
            low = work.tile([P, K], F32, name="low", bufs=4)
            dif = work.tile([P, K * NJ], F32, name="dif", bufs=4)
            fac = work.tile([P, K * NJ], F32, name="fac", bufs=4)
            fsum = work.tile([P, K * NJ], F32, name="fsum", bufs=4)
            tot = work.tile([P, K], F32, name="tot", bufs=4)
            rec = work.tile([P, K], F32, name="rec", bufs=4)
            pr = work.tile([P, K], F32, name="pr", bufs=4)
            alpha = work.tile([P, K * NJ], F32, name="alpha", bufs=4)
            st[nt] = dict(e=e_sb, negmax=negmax, sums=sums, low=low, dif=dif, fac=fac, fsum=fsum, tot=tot, rec=rec, pr=pr, alpha=alpha)

        def step(q, j):
            nt, k = divmod(q, K)
            if k == 0 and j == 0:
                begin(nt)
            s = st[nt]
            c = k * NJ + j
            cols = slice(j * CH, (j + 1) * CH)
            logits = lbank.tile([P, CH], F32, name="logits")
            nc.tensor.matmul_mx(
                out=logits[:],
                lhsT=a_codes[:, q * P : (q + 1) * P].bitcast(FP8X4),
                lhsT_scale=a_scales[:, q * P : (q + 1) * P],
                rhs=e_codes[:, cols].bitcast(FP8X4),
                rhs_scale=e_scales[:, cols],
                start=True,
                stop=True,
            )
            nc.vector.tensor_reduce(out=s["negmax"][:, c : c + 1], in_=logits[:], axis=AX.X, op=ALU.max, negate=True)
            nc.scalar.activation(
                out=s["e"][:, c, :],
                in_=logits[:],
                func=ACT.Exp,
                bias=s["negmax"][:, c : c + 1],
                accum_out=s["sums"][:, c : c + 1],
            )

        pis = {}

        def pi_a(nt):
            zneg = work.tile([P, 1], F32, name="zneg")
            ez = work.tile([P, K], F32, name="ez")
            zsum = work.tile([P, 1], F32, name="zsum")
            pi = work.tile([P, K], F32, name="pi")
            zcols = z_ps[:, nt * K * K : (nt + 1) * K * K : K + 1]
            nc.vector.tensor_reduce(out=zneg[:], in_=zcols, axis=AX.X, op=ALU.max, negate=True)
            nc.scalar.activation(out=ez[:], in_=zcols, func=ACT.Exp, bias=zneg[:], accum_out=zsum[:])
            pis[nt] = (ez, zsum, pi)

        def pi_b(nt):
            ez, zsum, pi = pis[nt]
            zrec = work.tile([P, 1], F32, name="zrec")
            nc.vector.reciprocal(out=zrec[:], in_=zsum[:])
            nc.vector.tensor_scalar(out=pi[:], in0=ez[:], scalar1=zrec[:], scalar2=None, op0=ALU.mult)

        def cube(tile, k0, k1):
            return tile[:, k0 * NJ : k1 * NJ].rearrange("p (k j) -> p k j", j=NJ)

        def chain_a(nt, k0, k1):
            s = st[nt]
            nc.vector.tensor_reduce(out=s["low"][:, k0:k1], in_=cube(s["negmax"], k0, k1), axis=AX.X, op=ALU.min)
            nc.vector.tensor_tensor(
                out=cube(s["dif"], k0, k1),
                in0=s["low"][:, k0:k1].unsqueeze(2).to_broadcast([P, k1 - k0, NJ]),
                in1=cube(s["negmax"], k0, k1),
                op=ALU.subtract,
            )
            nc.scalar.activation(out=s["fac"][:, k0 * NJ : k1 * NJ], in_=s["dif"][:, k0 * NJ : k1 * NJ], func=ACT.Exp)

        def chain_b(nt, k0, k1):
            s = st[nt]
            pi = pis[nt][2]
            cols = slice(k0 * NJ, k1 * NJ)
            nc.vector.tensor_tensor(out=s["fsum"][:, cols], in0=s["fac"][:, cols], in1=s["sums"][:, cols], op=ALU.mult)
            nc.vector.tensor_reduce(out=s["tot"][:, k0:k1], in_=cube(s["fsum"], k0, k1), axis=AX.X, op=ALU.add)
            nc.vector.reciprocal(out=s["rec"][:, k0:k1], in_=s["tot"][:, k0:k1])
            nc.vector.tensor_tensor(out=s["pr"][:, k0:k1], in0=s["rec"][:, k0:k1], in1=pi[:, k0:k1], op=ALU.mult)
            nc.vector.tensor_tensor(
                out=cube(s["alpha"], k0, k1),
                in0=cube(s["fac"], k0, k1),
                in1=s["pr"][:, k0:k1].unsqueeze(2).to_broadcast([P, k1 - k0, NJ]),
                op=ALU.mult,
            )

        diags = {}
        sums_ps = {}

        def build_diag(nt, j, ks):
            for k in ks:
                c = k * NJ + j
                diag = work.tile([P, P], F32, name="diag", bufs=12)
                diags[nt, c] = diag
                nc.gpsimd.tensor_scalar(
                    out=diag[:], in0=ident[:], scalar1=st[nt]["alpha"][:, c : c + 1], scalar2=0.0, op0=ALU.mult, op1=ALU.add
                )

        def mix(nt, j, k):
            m = ON_PE[nt][j]
            c = k * NJ + j
            cols = slice(j * CH, (j + 1) * CH)
            e = st[nt]["e"][:, c, :]
            weight = st[nt]["alpha"][:, c : c + 1]
            dst = acc[:, nt, cols]
            if k < m:
                if k == 0:
                    bank = xbank.tile([P, 512], F32, name="bank")
                    sums_ps[nt, j] = bank
                nc.tensor.matmul(sums_ps[nt, j][:], lhsT=diags[nt, c][:], rhs=e, start=(k == 0), stop=(k == m - 1))
                if k == K - 1:
                    nc.scalar.copy(out=dst, in_=sums_ps[nt, j][:])
            elif k == 0:
                nc.scalar.activation(out=dst, in_=e, func=ACT.Copy, scale=weight)
            else:
                nc.vector.scalar_tensor_tensor(
                    out=dst, in0=e, scalar=weight, in1=sums_ps[nt, j][:] if k == m else dst, op0=ALU.mult, op1=ALU.add
                )

        plan = {}

        def at(q, j, fn, *args):
            plan.setdefault((q, j), []).append((fn, args))

        widen(0, (0, 1))
        widen(0, (2, 3), False)
        turn_h()
        turn_gu()
        interleave(0)
        quant_w(0)
        turn_e(0)
        quant_h()
        context(0)
        quant_e(0)
        widen(1, (0, 1, 2, 3))
        gain(0)
        interleave(1)
        quant_a(0)
        turn_e(1)

        at(0, 0, quant_w, 1)
        at(0, 0, quant_e, 1)
        at(0, 0, context, 1)
        at(0, 0, turn_e, 2)
        at(0, 1, quant_e, 2)
        at(0, 1, gain, 1)
        at(0, 1, widen, 2, (0, 1))
        at(0, 1, turn_e, 3)
        at(0, 2, quant_e, 3)
        at(0, 2, quant_a, 1)
        at(0, 2, widen, 2, (2, 3))
        at(0, 3, interleave, 2)
        at(0, 3, mix_logit, 0)
        at(1, 0, quant_w, 2)
        at(1, 0, context, 2)
        at(1, 0, widen, 3, (0, 1))
        at(1, 1, widen, 3, (2, 3))
        at(1, 2, mix_logit, 1)
        at(1, 3, gain, 2)
        at(1, 3, interleave, 3)
        at(1, 3, quant_a, 2)
        at(2, 0, quant_w, 3)
        at(2, 0, context, 3)
        at(2, 1, context, 4)
        at(2, 1, mix_logit, 2)
        at(2, 2, gain, 3)
        at(2, 3, context, 5)
        at(2, 3, gain, 4)
        at(2, 3, quant_a, 3)
        at(3, 0, quant_a, 4)
        at(3, 0, mix_logit, 3)
        at(3, 1, gain, 5)
        at(3, 2, context, 6)
        at(3, 2, mix_logit, 4)
        at(3, 3, quant_a, 5)
        at(3, 3, mix_logit, 5)
        at(3, 3, gain, 6)
        at(3, 3, context, 7)
        at(3, 3, mix_logit, 6)
        for q in range(4, UNITS):
            at(q, 0, gain, q + 3)
            at(q, 0, context, q + 4)
            at(q, 2, quant_a, q + 3)
            at(q, 3, mix_logit, q + 3)
        for nt in range(NT):
            at(nt * K + 3, 1, pi_a, nt)
            at(nt * K + 3, 3, pi_b, nt)
        for nt in range(NT - 1):
            base = (nt + 1) * K
            at(base, 0, chain_a, nt, 0, K)
            at(base + 1, 0, chain_b, nt, 0, K)
            for j in range(NJ):
                at(base + 1, 0, build_diag, nt, j, range(ON_PE[nt][j]))
                for k in range(K):
                    when = base * NJ + LAG + 3 * j + k
                    at(when // NJ, when % NJ, mix, nt, j, k)
        last = NT - 1
        at(UNITS - 1, 0, chain_a, last, 0, K - 1)

        def run(q, j):
            for fn, args in plan.get((q, j), ()):
                fn(*args)

        for q in range(UNITS):
            for j in range(NJ):
                step(q, j)
                run(q, j)
        chain_a(last, K - 1, K)
        chain_b(last, 0, K - 1)
        for j in range(NJ):
            build_diag(last, j, range(ON_PE[last][j]))
        for extra in range(16):
            run(UNITS + extra // NJ, extra % NJ)
        vocab = keep.tile([P, 1], F32, name="vocab")
        nc.vector.tensor_scalar(out=vocab[:], in0=st[last]["fac"][:, K * NJ - 1 : K * NJ], scalar1=0.0, scalar2=float(V), op0=ALU.mult, op1=ALU.add)
        for nt in range(NT - 1):
            nc.scalar.activation(out=acc[:, nt, :], in_=acc[:, nt, :], func=ACT.Ln, scale=vocab[:])
        for j in range(NJ):
            for k in range(K - 1):
                mix(last, j, k)
        chain_b(last, K - 1, K)
        out_view = out.rearrange("(p t) v -> t p v", t=NT)
        for nt in range(NT - 1):
            nc.sync.dma_start(out=out_view[nt], in_=acc[:, nt, :])
        for j in range(NJ):
            cols = slice(j * CH, (j + 1) * CH)
            mix(last, j, K - 1)
            nc.scalar.activation(out=acc[:, last, cols], in_=acc[:, last, cols], func=ACT.Ln, scale=vocab[:])
            nc.sync.dma_start(out=out_view[last][:, cols], in_=acc[:, last, cols])
